import numpy as np
import ml_dtypes


def mxq(x, axis, fmt="e4m3"):
    dtype, down = {"e4m3": (ml_dtypes.float8_e4m3fn, 7), "e5m2": (ml_dtypes.float8_e5m2, 14)}[fmt]
    v = np.moveaxis(np.asarray(x, np.float32).astype(ml_dtypes.bfloat16).astype(np.float64), axis, -1)
    blocks = v.reshape(v.shape[:-1] + (-1, 32))
    amax = np.abs(blocks).max(-1, keepdims=True)
    byte = np.maximum(np.where(amax > 0, np.frexp(amax)[1] - 1 + 127, 0) - down, 1)
    scale = np.exp2(byte - 127.0)
    codes = (blocks / scale).astype(np.float32).astype(dtype).astype(np.float64)
    return np.moveaxis((codes * scale).reshape(v.shape), -1, axis)


WIDE = False


def mx_kscale(k):
    if not WIDE:
        return np.ones(k)
    levels = np.array([10, -10, 5, -5, 0])
    if k % 512:
        return np.exp2(np.random.permutation(np.resize(levels, k // 32))).repeat(32)
    a = np.empty((k // 512, 16))
    for p in range(k // 512):
        a[p, :8] = np.random.permutation(np.resize(levels, 8))
        for g in range(8):
            far = levels[np.abs(levels - a[p, g]) >= 10]
            a[p, g + 8] = far[np.random.randint(len(far))]
    return np.exp2(a.ravel()).repeat(32)


def f64(x):
    return np.asarray(x).astype(np.float64)


def striped(idx):
    return np.tile(idx.reshape(-1, 16).T, (8, 1)).astype(np.uint16)


def unstriped(offs):
    return offs[:16].T.reshape(-1).astype(np.int64)


def striped8(idx):
    return np.concatenate([x.reshape(-1, 16).T for x in idx]).astype(np.uint16)


def runs(offs, k):
    lists = np.stack([offs[16 * r : 16 * r + 16].T.reshape(-1) for r in range(8)]).astype(np.int64)
    return lists[np.arange(k) % 512 // 64]


def pack_weight(w):
    k, n = w.shape
    w = f64(np.asarray(w, np.float32).astype(ml_dtypes.bfloat16)).reshape(k // 32, 32, n)
    amax = np.abs(w).max(1)
    byte = np.clip(np.where(amax > 0, np.frexp(amax)[1] - 1 + 127 - 7, 1), 1, 254)
    scaled = (w * np.exp2(127.0 - byte)[:, None, :]).reshape(k, n).astype(np.float32)
    words = np.ascontiguousarray(scaled.reshape(k // 512, 128, 4, n).transpose(0, 1, 3, 2)).astype(ml_dtypes.float8_e4m3fn).view(np.uint8)
    return words, np.ascontiguousarray(byte.astype(np.uint8).reshape(k // 512, 16, n))


def unpack_weight(words, scales):
    g, p, n, _ = words.shape
    vals = np.ascontiguousarray(words).view(ml_dtypes.float8_e4m3fn).astype(np.float64) * np.repeat(np.exp2(scales.astype(np.float64) - 127.0), 8, axis=1)[..., None]
    return vals.transpose(0, 1, 3, 2).reshape(g * 512, n)


def relu(v):
    return np.maximum(v, 0.0)


def sigmoid(v):
    return 1.0 / (1.0 + np.exp(-np.maximum(v, -700.0)))


K, T, S, N, G, H = 512, 1024, 512, 512, 2048, 512


def setup_inputs():
    n = np.random.standard_normal
    s = mx_kscale(K)[:, None]
    u = mx_kscale(S)
    packed_xT = pack_weight(n((K, T)) * s)
    packed_dT = pack_weight(n((K, G)) / s)
    return {
        "x_words": packed_xT[0],
        "x_scales": packed_xT[1],
        "d_words": packed_dT[0],
        "d_scales": packed_dT[1],
        "gn": (np.random.uniform(0.5, 1.5, (H, 1)) * u[:, None]).astype(np.float32),
        "gm": (np.random.uniform(0.5, 1.5, (H, 1)) * u[:, None]).astype(np.float32),
        "w1": (n((H, N)) / np.sqrt(2 * H) / u[:, None]).astype(np.float32),
        "w2": (n((H, N)) / np.sqrt(2 * H) / u[:, None]).astype(np.float32),
        "offs": striped(np.random.permutation(T)[:S]),
        "k1": striped8(np.random.randint(0, G, (8, H))),
        "two": striped(np.random.permutation(T)[:S]),
        "n1": striped8(np.stack([np.random.permutation(S) for _ in range(8)])),
        "n2": striped8(np.stack([np.random.permutation(S) for _ in range(8)])),
        "n3": striped8(np.stack([np.random.permutation(S) for _ in range(8)])),
        "n4": striped8(np.stack([np.random.permutation(S) for _ in range(8)])),
        "n5": striped(np.random.permutation(S)),
        "n6": striped(np.random.permutation(S)),
        "n7": striped(np.random.permutation(S)),
    }


def reference(x_words, x_scales, d_words, d_scales, gn, gm, w1, w2, offs, k1, two, n1, n2, n3, n4, n5, n6, n7):
    d_k1 = unpack_weight(d_words, d_scales)[np.arange(K)[:, None], runs(k1, K)]
    xq = unpack_weight(x_words, x_scales)[:, unstriped(offs)]
    a = 0.0625 * (d_k1.T @ xq)
    z = f64(gn) * (relu(a - (a[np.arange(H)[:, None], runs(n1, H)])) + 0.5 * (relu(a[np.arange(H)[:, None], runs(n2, H)] - a)))
    x_two = unpack_weight(x_words, x_scales)[:, unstriped(two)]
    b = 0.0625 * (d_k1.T @ x_two)
    st = b[np.arange(H)[:, None], runs(n3, H)] - b
    z2 = f64(gm) * (b * (sigmoid(st[np.arange(H)[:, None], runs(n4, H)])))
    h = mxq(f64(w1), 0, "e4m3").T @ mxq(z, 0, "e4m3") + mxq(f64(w2), 0, "e4m3").T @ mxq(z2, 0, "e4m3")
    return np.maximum(h, h[:, unstriped(n5)]) - (np.maximum(h[:, unstriped(n6)], h[:, unstriped(n7)]))

@@ -1,0 +1,255 @@
+from contextlib import ExitStack
+
+import concourse.mybir as mybir
+
+K, T, S, N, G, H = 512, 1024, 512, 512, 2048, 512
+FLOPS = 4 * 2 * 512 * 512 * 512
+
+F32 = mybir.dt.float32
+BF16 = mybir.dt.bfloat16
+I32 = mybir.dt.int32
+U32 = mybir.dt.uint32
+U16 = mybir.dt.uint16
+U8 = mybir.dt.uint8
+FP8X4 = mybir.dt.float8_e4m3fn_x4
+ALU = mybir.AluOpType
+ACT = mybir.ActivationFunctionType
+
+P = 128
+PACK = 4
+WINDOW = 2 * S
+HALF = S // 2
+SCORE_SCALE = 0.0625
+
+
+def tile_picked_kjhingehopdmix_none_p_kernel(tc, x_words, x_scales, d_words, d_scales, gn, gm, w1, w2, offs, k1, two, n1, n2, n3, n4, n5, n6, n7, out):
+    nc = tc.nc
+    with ExitStack() as ctx:
+        keep = ctx.enter_context(tc.tile_pool(name="keep", bufs=1))
+        psum = ctx.enter_context(tc.psum_pool(name="psum", bufs=1))
+
+        def sb(name, shape, dtype):
+            return keep.tile(shape, dtype, name=name, align_bytes=64)
+
+        def load_list(name, dram):
+            tile = keep.tile([P, S // 16], U16, name=name)
+            nc.sync.dma_start(tile[:], dram)
+            return tile
+
+        def bank(number, name):
+            return psum.tile([P, S], F32, name=name, tag="bank%d" % number)
+
+        ds_table = sb("ds_table", [P, G], U8)
+        xs_table = sb("xs_table", [P, T], U8)
+        key_scales = sb("key_scales", [P, H], U8)
+        nc.vector.memset(ds_table[:].bitcast(I32), 0)
+        nc.vector.memset(xs_table[:].bitcast(I32), 0)
+        nc.vector.memset(key_scales[:].bitcast(I32), 0)
+
+        xw_table = sb("xw_table", [P, T], U32)
+        dw_table = sb("dw_table", [P, G], U32)
+        k1_l = load_list("k1_l", k1)
+        nc.sync.dma_start(ds_table[0:P:8, :].bitcast(I32), d_scales[0].bitcast(I32))
+        two_l = load_list("two_l", two)
+        nc.sync.dma_start(xw_table[:].bitcast(I32), x_words[0].rearrange("p n t -> p (n t)").bitcast(I32))
+        nc.sync.dma_start(dw_table[:].bitcast(I32), d_words[0].rearrange("p n t -> p (n t)").bitcast(I32))
+        for q in range(4):
+            nc.scalar.dma_start(xs_table[32 * q : 32 * q + 4, :].bitcast(I32), x_scales[0, 4 * q : 4 * q + 4, :].bitcast(I32))
+        offs_l = load_list("offs_l", offs)
+        w1_raw = [sb("w1_raw%d" % h, [P, PACK, HALF], F32) for h in range(2)]
+        w1_rows = w1.rearrange("(p t) n -> p t n", t=PACK)
+        for h in range(2):
+            nc.sync.dma_start(w1_raw[h][:], w1_rows[:, :, h * HALF : (h + 1) * HALF])
+        n3_l = load_list("n3_l", n3)
+        n1_l = load_list("n1_l", n1)
+        n2_l = load_list("n2_l", n2)
+        w2_raw = sb("w2_raw", [P, PACK, N], F32)
+        nc.sync.dma_start(w2_raw[:], w2.rearrange("(p t) n -> p t n", t=PACK))
+        n4_l = load_list("n4_l", n4)
+        gn_t = sb("gn_t", [P, PACK], F32)
+        gm_t = sb("gm_t", [P, PACK], F32)
+        nc.sync.dma_start(gn_t[:], gn.rearrange("(p t) o -> p (t o)", t=PACK))
+        nc.sync.dma_start(gm_t[:], gm.rearrange("(p t) o -> p (t o)", t=PACK))
+        n5_l = load_list("n5_l", n5)
+        n6_l = load_list("n6_l", n6)
+        n7_l = load_list("n7_l", n7)
+
+        ds_picked = sb("ds_picked", [P, H], U8)
+        ds_dealt = sb("ds_dealt", [P, H], U8)
+        nc.vector.tensor_copy(ds_picked[:], ds_table[:].indirect(k1_l[:]))
+        nc.vector.tensor_copy(ds_dealt[:].rearrange("p (t m) -> p m t", t=PACK), ds_picked[:].rearrange("p (m t) -> p m t", t=PACK))
+        for j in range(4):
+            nc.scalar.dma_start(key_scales[j:P:32, :].bitcast(I32), ds_dealt[8 * j : P : 32, :].bitcast(I32))
+
+        def pick_tokens(name, lst):
+            words = sb(name + "_words", [P, S], U32)
+            scales = sb(name + "_scales", [P, S], U8)
+            nc.vector.tensor_copy(scales[:], xs_table[:].indirect(lst[:]))
+            nc.vector.tensor_copy(words[:], xw_table[:].indirect(lst[:]))
+            return words, scales
+
+        xb_words, xb_scales = pick_tokens("xb", two_l)
+        dw_picked = sb("dw_picked", [P, H], U32)
+        key_words = sb("key_words", [P, H], U32)
+        nc.vector.tensor_copy(dw_picked[:], dw_table[:].indirect(k1_l[:]))
+        nc.vector.tensor_copy(key_words[:].rearrange("p (t m) -> p m t", t=PACK), dw_picked[:].rearrange("p (m t) -> p m t", t=PACK))
+        xa_words, xa_scales = pick_tokens("xa", offs_l)
+
+        def score(name, words, scales, first_bank):
+            windows = []
+            for t in range(PACK):
+                acc = bank(first_bank + t, "%s_acc%d" % (name, t))
+                cols = slice(t * P, (t + 1) * P)
+                nc.tensor.matmul_mx(out=acc[:], lhsT=key_words[:, cols].bitcast(FP8X4), lhsT_scale=key_scales[:, cols],
+                                    rhs=words[:].bitcast(FP8X4), rhs_scale=scales[:], start=True, stop=True)
+                windows.append((acc, sb("%s_win%d" % (name, t), [P, WINDOW], F32)))
+            return windows
+
+        def drain(pair):
+            nc.scalar.activation(pair[1][:, 0:S], pair[0][:], ACT.Copy, scale=SCORE_SCALE)
+
+        def interleave_view(ap):
+            return ap.rearrange("p (c i) t -> p c t i", i=4)
+
+        def plane_view(ap):
+            return ap.rearrange("p t (c i) -> p c t i", i=4)
+
+        w1_il = sb("w1_il", [P, N, PACK], BF16)
+        w2_il = sb("w2_il", [P, N, PACK], BF16)
+        for h in range(2):
+            nc.scalar.activation(interleave_view(w1_il[:, h * HALF : (h + 1) * HALF, :]), plane_view(w1_raw[h][:]), ACT.Copy)
+
+        b_pairs = score("b", xb_words, xb_scales, 0)
+        a_pairs = score("a", xa_words, xa_scales, 4)
+        b_win = [pair[1] for pair in b_pairs]
+        a_win = [pair[1] for pair in a_pairs]
+        st_win = [sb("st_win%d" % t, [P, WINDOW], F32) for t in range(PACK)]
+        g3 = [sb("g3_%d" % t, [P, S], F32) for t in range(PACK)]
+
+        def step(t):
+            nc.vector.tensor_tensor(st_win[t][:, 0:S], g3[t][:], b_win[t][:, 0:S], ALU.subtract)
+
+        half_gn = sb("half_gn", [P, PACK], F32)
+        nc.vector.tensor_scalar(half_gn[:], gn_t[:], 0.5, None, ALU.mult)
+        up = sb("up", [P, PACK, S], F32)
+        down = sb("down", [P, PACK, S], F32)
+
+        def a_step(t):
+            g1 = sb("g1_%d" % t, [P, S], F32)
+            g2 = sb("g2_%d" % t, [P, S], F32)
+            drain(a_pairs[t])
+            nc.scalar.activation(g1[:], a_win[t][:].indirect(n1_l[:]), ACT.Copy)
+            nc.scalar.activation(g2[:], a_win[t][:].indirect(n2_l[:]), ACT.Copy)
+            nc.vector.tensor_tensor(g1[:], a_win[t][:, 0:S], g1[:], ALU.subtract)
+            nc.vector.tensor_tensor(g2[:], g2[:], a_win[t][:, 0:S], ALU.subtract)
+            nc.vector.tensor_scalar(down[:, t, :], g1[:], 0.0, gn_t[:, t : t + 1], ALU.max, ALU.mult)
+            nc.vector.tensor_scalar(up[:, t, :], g2[:], 0.0, half_gn[:, t : t + 1], ALU.max, ALU.mult)
+
+        def quantise(name, il, width):
+            codes = sb(name + "_codes", [P, width], U32)
+            scales = sb(name + "_scales", [P, width], U8)
+            nc.vector.quantize_mx(out=codes[:].bitcast(FP8X4), scales=scales[:], in_=il[:].rearrange("p c t -> p (c t)"))
+            return codes, scales
+
+        for t in (0, 1):
+            drain(b_pairs[t])
+        for t in (0, 1):
+            nc.vector.tensor_copy(g3[t][:], b_win[t][:].indirect(n3_l[:]))
+        for t in (0, 1):
+            step(t)
+        a_step(0)
+        nc.vector.tensor_copy(interleave_view(w2_il[:]), plane_view(w2_raw[:]))
+        w1_q = quantise("w1", w1_il, N)
+        w2_q = quantise("w2", w2_il, N)
+        a_step(1)
+        a_step(2)
+        a_step(3)
+        for t in (2, 3):
+            drain(b_pairs[t])
+            nc.scalar.activation(g3[t][:], b_win[t][:].indirect(n3_l[:]), ACT.Copy)
+
+        z_il = sb("z_il", [P, S, PACK], BF16)
+        nc.vector.tensor_tensor(interleave_view(z_il[:]), plane_view(up[:]), plane_view(down[:]), ALU.add)
+        for t in (2, 3):
+            step(t)
+        z_q = quantise("z", z_il, S)
+
+        h_acc = [[psum.tile([P, HALF], F32, name="h_acc%d_%d" % (h, m), tag="bank%d" % (4 * (1 - h) + m)) for m in range(4)] for h in range(2)]
+        h_win = [sb("h_win%d" % m, [P, WINDOW], F32) for m in range(4)]
+
+        def h_pass(h, m, wq, codes, scales, first):
+            rows = slice(m * P, (m + 1) * P)
+            nc.tensor.matmul_mx(out=h_acc[h][m][:], lhsT=wq[0][:, rows].bitcast(FP8X4), lhsT_scale=wq[1][:, rows],
+                                rhs=codes.bitcast(FP8X4), rhs_scale=scales, start=first, stop=not first)
+
+        def h_drain(h, m):
+            nc.scalar.copy(h_win[m][:, h * HALF : (h + 1) * HALF], h_acc[h][m][:])
+
+        for h in range(2):
+            cols = slice(h * HALF, (h + 1) * HALF)
+            for m in range(4):
+                h_pass(h, m, w1_q, z_q[0][:, cols], z_q[1][:, cols], True)
+
+        z2_planes = [sb("z2_planes%d" % h, [P, PACK, HALF], BF16) for h in range(2)]
+        z2_il = [sb("z2_il%d" % h, [P, HALF, PACK], BF16) for h in range(2)]
+
+        def gate_plane(h, t):
+            gate = sb("gate%d_%d" % (h, t), [P, HALF], F32)
+            nc.scalar.activation(gate[:], st_win[t][:].indirect(n4_l[:, h * (HALF // 16) : (h + 1) * (HALF // 16)]), ACT.Sigmoid)
+            nc.vector.scalar_tensor_tensor(z2_planes[h][:, t, :], b_win[t][:, h * HALF : (h + 1) * HALF], gm_t[:, t : t + 1], gate[:], ALU.mult, ALU.mult)
+
+        def finish_half(h):
+            z2_q = quantise("z2_%d" % h, z2_il[h], HALF)
+            for m in range(4):
+                h_pass(h, m, w2_q, z2_q[0][:], z2_q[1][:], False)
+
+        for t in range(PACK):
+            gate_plane(0, t)
+        gate_plane(1, 0)
+        nc.vector.tensor_copy(interleave_view(z2_il[0][:]), plane_view(z2_planes[0][:]))
+        gate_plane(1, 1)
+        finish_half(0)
+        gate_plane(1, 2)
+        gate_plane(1, 3)
+        nc.vector.tensor_copy(interleave_view(z2_il[1][:]), plane_view(z2_planes[1][:]))
+        finish_half(1)
+        for m in range(4):
+            h_drain(0, m)
+
+        g5 = [sb("g5_%d" % m, [P, S], F32) for m in range(4)]
+        g6 = [sb("g6_%d" % m, [P, S], F32) for m in range(4)]
+        g7 = [sb("g7_%d" % m, [P, S], F32) for m in range(4)]
+
+        def fetch7(m):
+            h_drain(1, m)
+            nc.vector.tensor_copy(g7[m][:], h_win[m][:].indirect(n7_l[:]))
+
+        def larger67(m):
+            nc.scalar.activation(g6[m][:], h_win[m][:].indirect(n6_l[:]), ACT.Copy)
+            nc.vector.tensor_tensor(g6[m][:], g6[m][:], g7[m][:], ALU.max)
+
+        def larger5(m, cols):
+            nc.scalar.activation(g5[m][:, cols], h_win[m][:].indirect(n5_l[:, cols.start // 16 : cols.stop // 16]), ACT.Copy)
+            nc.vector.tensor_tensor(g5[m][:, cols], h_win[m][:, cols], g5[m][:, cols], ALU.max)
+
+        def finish(m, cols):
+            nc.vector.tensor_tensor(g7[m][:, cols], g5[m][:, cols], g6[m][:, cols], ALU.subtract)
+            nc.sync.dma_start(out[m * P : (m + 1) * P, cols], g7[m][:, cols])
+
+        whole = slice(0, S)
+        fetch7(0)
+        fetch7(1)
+        for m in range(2):
+            larger67(m)
+            larger5(m, whole)
+            fetch7(m + 2)
+            finish(m, whole)
+        larger67(2)
+        larger5(2, whole)
+        larger67(3)
+        finish(2, whole)
+        halves = [slice(0, HALF), slice(HALF, S)]
+        for cols in halves:
+            larger5(3, cols)
+        for cols in halves:
+            finish(3, cols)

@@ -39,6 +39,11 @@ def tile_picked_kjhingehopdmix_none_p_kernel(tc, x_words, x_scales, d_words, d_s
         def bank(number, name):
             return psum.tile([P, S], F32, name=name, tag="bank%d" % number)
 
+        warm_in = sb("warm_in", [P, 1], F32)
+        warm_out = sb("warm_out", [P, 1], F32)
+        nc.vector.memset(warm_in[:], 0.0)
+        nc.scalar.activation(warm_out[:], warm_in[:], ACT.Sigmoid)
+
         ds_table = sb("ds_table", [P, G], U8)
         xs_table = sb("xs_table", [P, T], U8)
         key_scales = sb("key_scales", [P, H], U8)

@@ -20,16 +20,23 @@ PACK = 4
 WINDOW = 2 * S
 HALF = S // 2
 SCORE_SCALE = 0.0625
+WINDOW_BYTES = 4 * WINDOW
+B_WINDOWS = 4 * G + 4 * H
+LARGE = 2.0 ** 126
 
 
 def tile_picked_kjhingehopdmix_none_p_kernel(tc, x_words, x_scales, d_words, d_scales, gn, gm, w1, w2, offs, k1, two, n1, n2, n3, n4, n5, n6, n7, out):
     nc = tc.nc
     with ExitStack() as ctx:
         keep = ctx.enter_context(tc.tile_pool(name="keep", bufs=1))
+        reuse = ctx.enter_context(tc.tile_pool(name="reuse", bufs=1))
         psum = ctx.enter_context(tc.psum_pool(name="psum", bufs=1))
 
-        def sb(name, shape, dtype):
-            return keep.tile(shape, dtype, name=name, align_bytes=64)
+        def sb(name, shape, dtype, tag=""):
+            return keep.tile(shape, dtype, name=name, tag=tag or name, align_bytes=64)
+
+        def placed(name, shape, dtype, offset):
+            return reuse.tile(shape, dtype, name=name, align_bytes=64, offset=offset)
 
         def load_list(name, dram):
             tile = keep.tile([P, S // 16], U16, name=name)
@@ -39,111 +46,125 @@ def tile_picked_kjhingehopdmix_none_p_kernel(tc, x_words, x_scales, d_words, d_s
         def bank(number, name):
             return psum.tile([P, S], F32, name=name, tag="bank%d" % number)
 
-        warm_in = sb("warm_in", [P, 1], F32)
-        warm_out = sb("warm_out", [P, 1], F32)
-        nc.vector.memset(warm_in[:], 0.0)
-        nc.scalar.activation(warm_out[:], warm_in[:], ACT.Sigmoid)
-
         ds_table = sb("ds_table", [P, G], U8)
         xs_table = sb("xs_table", [P, T], U8)
-        key_scales = sb("key_scales", [P, H], U8)
         nc.vector.memset(ds_table[:].bitcast(I32), 0)
+        warm_in = sb("warm_in", [P, 1], F32)
+        warm_out = sb("warm_out", [P, 1], F32)
+        nc.gpsimd.memset(warm_in[:], 0.0)
+        nc.scalar.activation(warm_out[:], warm_in[:], ACT.Sigmoid)
         nc.vector.memset(xs_table[:].bitcast(I32), 0)
-        nc.vector.memset(key_scales[:].bitcast(I32), 0)
 
         xw_table = sb("xw_table", [P, T], U32)
-        dw_table = sb("dw_table", [P, G], U32)
+        dw_table = placed("dw_table", [P, G], U32, 0)
+        w1_rows = w1.rearrange("(p t) n -> p t n", t=PACK)
+        w1_raw = [placed("w1_raw%d" % h, [P, PACK, HALF], F32, B_WINDOWS + (2 * (1 - h) + 1) * WINDOW_BYTES - WINDOW_BYTES // 2) for h in range(2)]
+        w2_raw = sb("w2_raw", [P, PACK, N], F32)
+        gn_t = sb("gn_t", [P, PACK], F32)
+        gm_t = sb("gm_t", [P, PACK], F32)
+
         k1_l = load_list("k1_l", k1)
         nc.sync.dma_start(ds_table[0:P:8, :].bitcast(I32), d_scales[0].bitcast(I32))
         two_l = load_list("two_l", two)
-        nc.sync.dma_start(xw_table[:].bitcast(I32), x_words[0].rearrange("p n t -> p (n t)").bitcast(I32))
-        nc.sync.dma_start(dw_table[:].bitcast(I32), d_words[0].rearrange("p n t -> p (n t)").bitcast(I32))
         for q in range(4):
-            nc.scalar.dma_start(xs_table[32 * q : 32 * q + 4, :].bitcast(I32), x_scales[0, 4 * q : 4 * q + 4, :].bitcast(I32))
+            nc.sync.dma_start(xs_table[32 * q : 32 * q + 4, :].bitcast(I32), x_scales[0, 4 * q : 4 * q + 4, :].bitcast(I32))
+        nc.sync.dma_start(dw_table[:].bitcast(I32), d_words[0].rearrange("p n t -> p (n t)").bitcast(I32))
+        nc.sync.dma_start(xw_table[:].bitcast(I32), x_words[0].rearrange("p n t -> p (n t)").bitcast(I32))
         offs_l = load_list("offs_l", offs)
-        w1_raw = [sb("w1_raw%d" % h, [P, PACK, HALF], F32) for h in range(2)]
-        w1_rows = w1.rearrange("(p t) n -> p t n", t=PACK)
-        for h in range(2):
-            nc.sync.dma_start(w1_raw[h][:], w1_rows[:, :, h * HALF : (h + 1) * HALF])
+        nc.sync.dma_start(w1_raw[0][:], w1_rows[:, :, 0:HALF])
+        nc.sync.dma_start(w1_raw[1][:], w1_rows[:, :, HALF:N])
         n3_l = load_list("n3_l", n3)
         n1_l = load_list("n1_l", n1)
         n2_l = load_list("n2_l", n2)
-        w2_raw = sb("w2_raw", [P, PACK, N], F32)
         nc.sync.dma_start(w2_raw[:], w2.rearrange("(p t) n -> p t n", t=PACK))
         n4_l = load_list("n4_l", n4)
-        gn_t = sb("gn_t", [P, PACK], F32)
-        gm_t = sb("gm_t", [P, PACK], F32)
-        nc.sync.dma_start(gn_t[:], gn.rearrange("(p t) o -> p (t o)", t=PACK))
-        nc.sync.dma_start(gm_t[:], gm.rearrange("(p t) o -> p (t o)", t=PACK))
         n5_l = load_list("n5_l", n5)
         n6_l = load_list("n6_l", n6)
         n7_l = load_list("n7_l", n7)
+        nc.gpsimd.dma_start(gm_t[:], gm.rearrange("(p t) o -> p (t o)", t=PACK))
+        nc.gpsimd.dma_start(gn_t[:], gn.rearrange("(p t) o -> p (t o)", t=PACK))
 
         ds_picked = sb("ds_picked", [P, H], U8)
-        ds_dealt = sb("ds_dealt", [P, H], U8)
+        key_scales = sb("key_scales", [P, H], U8)
         nc.vector.tensor_copy(ds_picked[:], ds_table[:].indirect(k1_l[:]))
-        nc.vector.tensor_copy(ds_dealt[:].rearrange("p (t m) -> p m t", t=PACK), ds_picked[:].rearrange("p (m t) -> p m t", t=PACK))
-        for j in range(4):
-            nc.scalar.dma_start(key_scales[j:P:32, :].bitcast(I32), ds_dealt[8 * j : P : 32, :].bitcast(I32))
+        nc.vector.tensor_copy(key_scales[:].rearrange("p (t m) -> p m t", t=PACK), ds_picked[:].rearrange("p (m t) -> p m t", t=PACK))
+        for j in range(1, 4):
+            nc.scalar.dma_start(key_scales[j:P:32, :].bitcast(I32), key_scales[8 * j : P : 32, :].bitcast(I32))
 
-        def pick_tokens(name, lst):
-            words = sb(name + "_words", [P, S], U32)
-            scales = sb(name + "_scales", [P, S], U8)
-            nc.vector.tensor_copy(scales[:], xs_table[:].indirect(lst[:]))
-            nc.vector.tensor_copy(words[:], xw_table[:].indirect(lst[:]))
-            return words, scales
-
-        xb_words, xb_scales = pick_tokens("xb", two_l)
-        dw_picked = sb("dw_picked", [P, H], U32)
+        xb_scales = sb("xb_scales", [P, S], U8)
+        nc.vector.tensor_copy(xb_scales[:], xs_table[:].indirect(two_l[:]))
+        dw_picked = placed("dw_picked", [P, H], U32, 4 * G)
         key_words = sb("key_words", [P, H], U32)
         nc.vector.tensor_copy(dw_picked[:], dw_table[:].indirect(k1_l[:]))
+        xb_words = placed("xb_words", [P, S], U32, 0)
+        nc.vector.tensor_copy(xb_words[:], xw_table[:].indirect(two_l[:]))
         nc.vector.tensor_copy(key_words[:].rearrange("p (t m) -> p m t", t=PACK), dw_picked[:].rearrange("p (m t) -> p m t", t=PACK))
-        xa_words, xa_scales = pick_tokens("xa", offs_l)
+        xa_words = placed("xa_words", [P, S], U32, 4 * G)
+        xa_scales = placed("xa_scales", [P, S], U8, 4 * S)
+        nc.vector.tensor_copy(xa_words[:], xw_table[:].indirect(offs_l[:]))
+        nc.vector.tensor_copy(xa_scales[:], xs_table[:].indirect(offs_l[:]))
 
-        def score(name, words, scales, first_bank):
-            windows = []
+        def score(name, words, scales, windows):
+            pairs = []
             for t in range(PACK):
-                acc = bank(first_bank + t, "%s_acc%d" % (name, t))
+                acc = bank(t, "%s_acc%d" % (name, t))
                 cols = slice(t * P, (t + 1) * P)
                 nc.tensor.matmul_mx(out=acc[:], lhsT=key_words[:, cols].bitcast(FP8X4), lhsT_scale=key_scales[:, cols],
                                     rhs=words[:].bitcast(FP8X4), rhs_scale=scales[:], start=True, stop=True)
-                windows.append((acc, sb("%s_win%d" % (name, t), [P, WINDOW], F32)))
-            return windows
+                pairs.append((acc, windows[t]))
+            return pairs
 
-        def drain(pair):
-            nc.scalar.activation(pair[1][:, 0:S], pair[0][:], ACT.Copy, scale=SCORE_SCALE)
+        def drain(pair, scale):
+            nc.scalar.activation(pair[1][:, 0:S], pair[0][:], ACT.Copy, scale=scale)
+
+        b_scale = sb("b_scale", [P, PACK], F32)
+        gm_safe = sb("gm_safe", [P, PACK], F32)
+        gm_inverse = sb("gm_inverse", [P, PACK], F32)
+        gm_zero = sb("gm_zero", [P, PACK], F32)
+        gm_recip = sb("gm_recip", [P, PACK], F32)
+        nc.gpsimd.tensor_scalar(b_scale[:], gm_t[:], SCORE_SCALE, 0.0, ALU.mult, ALU.add)
+        nc.gpsimd.tensor_scalar(gm_zero[:], gm_t[:], 0.0, 1.0, ALU.is_equal, ALU.mult)
+        nc.gpsimd.tensor_tensor(gm_safe[:], gm_t[:], gm_zero[:], ALU.add)
+        nc.vector.reciprocal(gm_recip[:], gm_safe[:])
+        nc.gpsimd.tensor_scalar(gm_inverse[:], gm_recip[:], LARGE, -LARGE, ALU.min, ALU.max)
 
         def interleave_view(ap):
-            return ap.rearrange("p (c i) t -> p c t i", i=4)
+            return ap.rearrange("p (c i) t -> p c t i", i=2)
 
         def plane_view(ap):
-            return ap.rearrange("p t (c i) -> p c t i", i=4)
+            return ap.rearrange("p t (c i) -> p c t i", i=2)
 
         w1_il = sb("w1_il", [P, N, PACK], BF16)
         w2_il = sb("w2_il", [P, N, PACK], BF16)
         for h in range(2):
             nc.scalar.activation(interleave_view(w1_il[:, h * HALF : (h + 1) * HALF, :]), plane_view(w1_raw[h][:]), ACT.Copy)
 
-        b_pairs = score("b", xb_words, xb_scales, 0)
-        a_pairs = score("a", xa_words, xa_scales, 4)
-        b_win = [pair[1] for pair in b_pairs]
-        a_win = [pair[1] for pair in a_pairs]
+        b_win = [placed("b_win%d" % t, [P, WINDOW], F32, B_WINDOWS + t * WINDOW_BYTES) for t in range(PACK)]
+        a_win = [sb("a_win%d" % t, [P, WINDOW], F32) for t in range(PACK)]
+        b_pairs = score("b", xb_words, xb_scales, b_win)
         st_win = [sb("st_win%d" % t, [P, WINDOW], F32) for t in range(PACK)]
         g3 = [sb("g3_%d" % t, [P, S], F32) for t in range(PACK)]
+
+        b_planes = sb("b_planes", [P, PACK, S], F32)
+
+        def drain_b(t):
+            drain(b_pairs[t], b_scale[:, t : t + 1])
+            nc.sync.dma_start(b_planes[:, t, :], b_win[t][:, 0:S])
 
         def step(t):
             nc.vector.tensor_tensor(st_win[t][:, 0:S], g3[t][:], b_win[t][:, 0:S], ALU.subtract)
 
         half_gn = sb("half_gn", [P, PACK], F32)
-        nc.vector.tensor_scalar(half_gn[:], gn_t[:], 0.5, None, ALU.mult)
+        nc.gpsimd.tensor_scalar(half_gn[:], gn_t[:], 0.5, 0.0, ALU.mult, ALU.add)
         up = sb("up", [P, PACK, S], F32)
         down = sb("down", [P, PACK, S], F32)
 
         def a_step(t):
             g1 = sb("g1_%d" % t, [P, S], F32)
             g2 = sb("g2_%d" % t, [P, S], F32)
-            drain(a_pairs[t])
             nc.scalar.activation(g1[:], a_win[t][:].indirect(n1_l[:]), ACT.Copy)
+            if t + 1 < PACK:
+                drain(a_pairs[t + 1], SCORE_SCALE)
             nc.scalar.activation(g2[:], a_win[t][:].indirect(n2_l[:]), ACT.Copy)
             nc.vector.tensor_tensor(g1[:], a_win[t][:, 0:S], g1[:], ALU.subtract)
             nc.vector.tensor_tensor(g2[:], g2[:], a_win[t][:, 0:S], ALU.subtract)
@@ -156,11 +177,15 @@ def tile_picked_kjhingehopdmix_none_p_kernel(tc, x_words, x_scales, d_words, d_s
             nc.vector.quantize_mx(out=codes[:].bitcast(FP8X4), scales=scales[:], in_=il[:].rearrange("p c t -> p (c t)"))
             return codes, scales
 
-        for t in (0, 1):
-            drain(b_pairs[t])
-        for t in (0, 1):
+        for t in range(PACK):
+            drain_b(t)
+        a_pairs = score("a", xa_words, xa_scales, a_win)
+        drain(a_pairs[0], SCORE_SCALE)
+        nc.scalar.activation(g3[3][:, HALF:S], b_win[3][:].indirect(n3_l[:, HALF // 16 : S // 16]), ACT.Copy)
+        for t in range(3):
             nc.vector.tensor_copy(g3[t][:], b_win[t][:].indirect(n3_l[:]))
-        for t in (0, 1):
+        nc.vector.tensor_copy(g3[3][:, 0:HALF], b_win[3][:].indirect(n3_l[:, 0 : HALF // 16]))
+        for t in range(PACK):
             step(t)
         a_step(0)
         nc.vector.tensor_copy(interleave_view(w2_il[:]), plane_view(w2_raw[:]))
@@ -169,15 +194,9 @@ def tile_picked_kjhingehopdmix_none_p_kernel(tc, x_words, x_scales, d_words, d_s
         a_step(1)
         a_step(2)
         a_step(3)
-        for t in (2, 3):
-            drain(b_pairs[t])
-            nc.scalar.activation(g3[t][:], b_win[t][:].indirect(n3_l[:]), ACT.Copy)
 
         z_il = sb("z_il", [P, S, PACK], BF16)
         nc.vector.tensor_tensor(interleave_view(z_il[:]), plane_view(up[:]), plane_view(down[:]), ALU.add)
-        for t in (2, 3):
-            step(t)
-        z_q = quantise("z", z_il, S)
 
         h_acc = [[psum.tile([P, HALF], F32, name="h_acc%d_%d" % (h, m), tag="bank%d" % (4 * (1 - h) + m)) for m in range(4)] for h in range(2)]
         h_win = [sb("h_win%d" % m, [P, WINDOW], F32) for m in range(4)]
@@ -190,34 +209,28 @@ def tile_picked_kjhingehopdmix_none_p_kernel(tc, x_words, x_scales, d_words, d_s
         def h_drain(h, m):
             nc.scalar.copy(h_win[m][:, h * HALF : (h + 1) * HALF], h_acc[h][m][:])
 
+        def gated_half(h):
+            gates = sb("gates%d" % h, [P, PACK, HALF], F32)
+            z2_il = sb("z2_il%d" % h, [P, HALF, PACK], BF16)
+            for t in range(PACK):
+                nc.scalar.activation(gates[:, t, :], st_win[t][:].indirect(n4_l[:, h * (HALF // 16) : (h + 1) * (HALF // 16)]), ACT.Sigmoid,
+                                     scale=gm_inverse[:, t : t + 1])
+            nc.vector.tensor_tensor(interleave_view(z2_il[:]), plane_view(b_planes[:, :, h * HALF : (h + 1) * HALF]), plane_view(gates[:]), ALU.mult)
+            return z2_il
+
+        def close_half(h, z2_il):
+            z2_q = quantise("z2_%d" % h, z2_il, HALF)
+            for m in range(4):
+                h_pass(h, m, w2_q, z2_q[0][:], z2_q[1][:], False)
+
+        z2_first = gated_half(0)
+        z_q = quantise("z", z_il, S)
         for h in range(2):
             cols = slice(h * HALF, (h + 1) * HALF)
             for m in range(4):
                 h_pass(h, m, w1_q, z_q[0][:, cols], z_q[1][:, cols], True)
-
-        z2_planes = [sb("z2_planes%d" % h, [P, PACK, HALF], BF16) for h in range(2)]
-        z2_il = [sb("z2_il%d" % h, [P, HALF, PACK], BF16) for h in range(2)]
-
-        def gate_plane(h, t):
-            gate = sb("gate%d_%d" % (h, t), [P, HALF], F32)
-            nc.scalar.activation(gate[:], st_win[t][:].indirect(n4_l[:, h * (HALF // 16) : (h + 1) * (HALF // 16)]), ACT.Sigmoid)
-            nc.vector.scalar_tensor_tensor(z2_planes[h][:, t, :], b_win[t][:, h * HALF : (h + 1) * HALF], gm_t[:, t : t + 1], gate[:], ALU.mult, ALU.mult)
-
-        def finish_half(h):
-            z2_q = quantise("z2_%d" % h, z2_il[h], HALF)
-            for m in range(4):
-                h_pass(h, m, w2_q, z2_q[0][:], z2_q[1][:], False)
-
-        for t in range(PACK):
-            gate_plane(0, t)
-        gate_plane(1, 0)
-        nc.vector.tensor_copy(interleave_view(z2_il[0][:]), plane_view(z2_planes[0][:]))
-        gate_plane(1, 1)
-        finish_half(0)
-        gate_plane(1, 2)
-        gate_plane(1, 3)
-        nc.vector.tensor_copy(interleave_view(z2_il[1][:]), plane_view(z2_planes[1][:]))
-        finish_half(1)
+        close_half(0, z2_first)
+        close_half(1, gated_half(1))
         for m in range(4):
             h_drain(0, m)
 

@@ -135,7 +135,6 @@ def tile_picked_kjhingehopdmix_none_p_kernel(tc, x_words, x_scales, d_words, d_s
             return ap.rearrange("p t (c i) -> p c t i", i=2)
 
         w1_il = sb("w1_il", [P, N, PACK], BF16)
-        w2_il = sb("w2_il", [P, N, PACK], BF16)
         for h in range(2):
             nc.scalar.activation(interleave_view(w1_il[:, h * HALF : (h + 1) * HALF, :]), plane_view(w1_raw[h][:]), ACT.Copy)
 
@@ -188,9 +187,7 @@ def tile_picked_kjhingehopdmix_none_p_kernel(tc, x_words, x_scales, d_words, d_s
         for t in range(PACK):
             step(t)
         a_step(0)
-        nc.vector.tensor_copy(interleave_view(w2_il[:]), plane_view(w2_raw[:]))
         w1_q = quantise("w1", w1_il, N)
-        w2_q = quantise("w2", w2_il, N)
         a_step(1)
         a_step(2)
         a_step(3)
@@ -198,48 +195,47 @@ def tile_picked_kjhingehopdmix_none_p_kernel(tc, x_words, x_scales, d_words, d_s
         z_il = sb("z_il", [P, S, PACK], BF16)
         nc.vector.tensor_tensor(interleave_view(z_il[:]), plane_view(up[:]), plane_view(down[:]), ALU.add)
 
-        h_acc = [[psum.tile([P, HALF], F32, name="h_acc%d_%d" % (h, m), tag="bank%d" % (4 * (1 - h) + m)) for m in range(4)] for h in range(2)]
+        h_acc = [bank(PACK + m, "h_acc%d" % m) for m in range(4)]
         h_win = [sb("h_win%d" % m, [P, WINDOW], F32) for m in range(4)]
 
-        def h_pass(h, m, wq, codes, scales, first):
-            rows = slice(m * P, (m + 1) * P)
-            nc.tensor.matmul_mx(out=h_acc[h][m][:], lhsT=wq[0][:, rows].bitcast(FP8X4), lhsT_scale=wq[1][:, rows],
-                                rhs=codes.bitcast(FP8X4), rhs_scale=scales, start=first, stop=not first)
-
-        def h_drain(h, m):
-            nc.scalar.copy(h_win[m][:, h * HALF : (h + 1) * HALF], h_acc[h][m][:])
+        def h_pass(m, cols, w_q, w_first, z_pair, start, stop):
+            rows = slice(m * P - w_first, (m + 1) * P - w_first)
+            nc.tensor.matmul_mx(out=h_acc[m][:, cols], lhsT=w_q[0][:, rows].bitcast(FP8X4), lhsT_scale=w_q[1][:, rows],
+                                rhs=z_pair[0][:].bitcast(FP8X4), rhs_scale=z_pair[1][:], start=start, stop=stop)
 
         def gated_half(h):
             gates = sb("gates%d" % h, [P, PACK, HALF], F32)
-            z2_il = sb("z2_il%d" % h, [P, HALF, PACK], BF16)
+            rounded = sb("z2_il%d" % h, [P, HALF, PACK], BF16)
             for t in range(PACK):
                 nc.scalar.activation(gates[:, t, :], st_win[t][:].indirect(n4_l[:, h * (HALF // 16) : (h + 1) * (HALF // 16)]), ACT.Sigmoid,
                                      scale=gm_inverse[:, t : t + 1])
-            nc.vector.tensor_tensor(interleave_view(z2_il[:]), plane_view(b_planes[:, :, h * HALF : (h + 1) * HALF]), plane_view(gates[:]), ALU.mult)
-            return z2_il
+            nc.vector.tensor_tensor(interleave_view(rounded[:]), plane_view(b_planes[:, :, h * HALF : (h + 1) * HALF]), plane_view(gates[:]), ALU.mult)
+            return rounded
 
-        def close_half(h, z2_il):
-            z2_q = quantise("z2_%d" % h, z2_il, HALF)
-            for m in range(4):
-                h_pass(h, m, w2_q, z2_q[0][:], z2_q[1][:], False)
-
-        z2_first = gated_half(0)
+        whole = slice(0, S)
+        halves = [slice(0, HALF), slice(HALF, S)]
+        z2_il = [gated_half(0)]
         z_q = quantise("z", z_il, S)
-        for h in range(2):
-            cols = slice(h * HALF, (h + 1) * HALF)
-            for m in range(4):
-                h_pass(h, m, w1_q, z_q[0][:, cols], z_q[1][:, cols], True)
-        close_half(0, z2_first)
-        close_half(1, gated_half(1))
         for m in range(4):
-            h_drain(0, m)
+            h_pass(m, whole, w1_q, 0, z_q, True, False)
+        z2_q = [quantise("z2_0", z2_il[0], HALF)]
+        z2_il.append(gated_half(1))
+        w2_il = [sb("w2_il%d" % h, [P, HALF, PACK], BF16, tag="st_win%d" % (3 - h)) for h in range(2)]
+        for h in range(2):
+            nc.scalar.activation(interleave_view(w2_il[h][:]), plane_view(w2_raw[:, :, halves[h]]), ACT.Copy)
+        w2_q = [quantise("w2_0", w2_il[0], HALF)]
+        z2_q.append(quantise("z2_1", z2_il[1], HALF))
+        w2_q.append(quantise("w2_1", w2_il[1], HALF))
+        for m in range(4):
+            for h in range(2):
+                h_pass(m, halves[h], w2_q[m // 2], (m // 2) * HALF, z2_q[h], False, h == 1)
 
         g5 = [sb("g5_%d" % m, [P, S], F32) for m in range(4)]
         g6 = [sb("g6_%d" % m, [P, S], F32) for m in range(4)]
         g7 = [sb("g7_%d" % m, [P, S], F32) for m in range(4)]
 
         def fetch7(m):
-            h_drain(1, m)
+            nc.scalar.copy(h_win[m][:, 0:S], h_acc[m][:])
             nc.vector.tensor_copy(g7[m][:], h_win[m][:].indirect(n7_l[:]))
 
         def larger67(m):
@@ -254,7 +250,6 @@ def tile_picked_kjhingehopdmix_none_p_kernel(tc, x_words, x_scales, d_words, d_s
             nc.vector.tensor_tensor(g7[m][:, cols], g5[m][:, cols], g6[m][:, cols], ALU.subtract)
             nc.sync.dma_start(out[m * P : (m + 1) * P, cols], g7[m][:, cols])
 
-        whole = slice(0, S)
         fetch7(0)
         fetch7(1)
         for m in range(2):
@@ -266,7 +261,6 @@ def tile_picked_kjhingehopdmix_none_p_kernel(tc, x_words, x_scales, d_words, d_s
         larger5(2, whole)
         larger67(3)
         finish(2, whole)
-        halves = [slice(0, HALF), slice(HALF, S)]
         for cols in halves:
             larger5(3, cols)
         for cols in halves:

@@ -3,7 +3,7 @@ from contextlib import ExitStack
 import concourse.mybir as mybir
 
 K, T, S, N, G, H = 512, 1024, 512, 512, 2048, 512
-FLOPS = 4 * 2 * 512 * 512 * 512
+FLOPS = 2 * (2 * K * H * S) + 2 * (2 * H * N * S)
 
 F32 = mybir.dt.float32
 BF16 = mybir.dt.bfloat16
@@ -17,15 +17,25 @@ ACT = mybir.ActivationFunctionType
 
 P = 128
 PACK = 4
+QUADRANT = 32
+BLOCK_PARTITIONS = 8
+GROUP = 16
+OUT_TILES = N // P
 WINDOW = 2 * S
 HALF = S // 2
 SCORE_SCALE = 0.0625
-WINDOW_BYTES = 4 * WINDOW
-B_WINDOWS = 4 * G + 4 * H
 LARGE = 2.0 ** 126
 
+WORD_BYTES = 4
+WINDOW_BYTES = WORD_BYTES * WINDOW
+DICTIONARY_AT = 0
+PICKED_KEYS_AT = DICTIONARY_AT + WORD_BYTES * G
+B_WINDOWS_AT = PICKED_KEYS_AT + WORD_BYTES * H
 
-def tile_picked_kjhingehopdmix_none_p_kernel(tc, x_words, x_scales, d_words, d_scales, gn, gm, w1, w2, offs, k1, two, n1, n2, n3, n4, n5, n6, n7, out):
+
+def tile_picked_kjhingehopdmix_none_p_kernel(
+    tc, x_words, x_scales, d_words, d_scales, gn, gm, w1, w2, offs, k1, two, n1, n2, n3, n4, n5, n6, n7, out
+):
     nc = tc.nc
     with ExitStack() as ctx:
         keep = ctx.enter_context(tc.tile_pool(name="keep", bufs=1))
@@ -39,12 +49,18 @@ def tile_picked_kjhingehopdmix_none_p_kernel(tc, x_words, x_scales, d_words, d_s
             return reuse.tile(shape, dtype, name=name, align_bytes=64, offset=offset)
 
         def load_list(name, dram):
-            tile = keep.tile([P, S // 16], U16, name=name)
+            tile = keep.tile([P, S // GROUP], U16, name=name)
             nc.sync.dma_start(tile[:], dram)
             return tile
 
+        def entries(lst, cols):
+            return lst[:, cols.start // GROUP : cols.stop // GROUP]
+
         def bank(number, name):
             return psum.tile([P, S], F32, name=name, tag="bank%d" % number)
+
+        whole = slice(0, S)
+        halves = [slice(0, HALF), slice(HALF, S)]
 
         ds_table = sb("ds_table", [P, G], U8)
         xs_table = sb("xs_table", [P, T], U8)
@@ -56,23 +72,28 @@ def tile_picked_kjhingehopdmix_none_p_kernel(tc, x_words, x_scales, d_words, d_s
         nc.vector.memset(xs_table[:].bitcast(I32), 0)
 
         xw_table = sb("xw_table", [P, T], U32)
-        dw_table = placed("dw_table", [P, G], U32, 0)
+        dw_table = placed("dw_table", [P, G], U32, DICTIONARY_AT)
         w1_rows = w1.rearrange("(p t) n -> p t n", t=PACK)
-        w1_raw = [placed("w1_raw%d" % h, [P, PACK, HALF], F32, B_WINDOWS + (2 * (1 - h) + 1) * WINDOW_BYTES - WINDOW_BYTES // 2) for h in range(2)]
+        w1_raw = [
+            placed("w1_raw%d" % h, [P, PACK, HALF], F32, B_WINDOWS_AT + 2 * (1 - h) * WINDOW_BYTES + WINDOW_BYTES // 2)
+            for h in range(2)
+        ]
         w2_raw = sb("w2_raw", [P, PACK, N], F32)
         gn_t = sb("gn_t", [P, PACK], F32)
         gm_t = sb("gm_t", [P, PACK], F32)
 
         k1_l = load_list("k1_l", k1)
-        nc.sync.dma_start(ds_table[0:P:8, :].bitcast(I32), d_scales[0].bitcast(I32))
+        nc.sync.dma_start(ds_table[0:P:BLOCK_PARTITIONS, :].bitcast(I32), d_scales[0].bitcast(I32))
         two_l = load_list("two_l", two)
-        for q in range(4):
-            nc.sync.dma_start(xs_table[32 * q : 32 * q + 4, :].bitcast(I32), x_scales[0, 4 * q : 4 * q + 4, :].bitcast(I32))
+        for q in range(P // QUADRANT):
+            nc.sync.dma_start(
+                xs_table[QUADRANT * q : QUADRANT * q + 4, :].bitcast(I32), x_scales[0, 4 * q : 4 * q + 4, :].bitcast(I32)
+            )
         nc.sync.dma_start(dw_table[:].bitcast(I32), d_words[0].rearrange("p n t -> p (n t)").bitcast(I32))
         nc.sync.dma_start(xw_table[:].bitcast(I32), x_words[0].rearrange("p n t -> p (n t)").bitcast(I32))
         offs_l = load_list("offs_l", offs)
-        nc.sync.dma_start(w1_raw[0][:], w1_rows[:, :, 0:HALF])
-        nc.sync.dma_start(w1_raw[1][:], w1_rows[:, :, HALF:N])
+        for h in range(2):
+            nc.sync.dma_start(w1_raw[h][:], w1_rows[:, :, halves[h]])
         n3_l = load_list("n3_l", n3)
         n1_l = load_list("n1_l", n1)
         n2_l = load_list("n2_l", n2)
@@ -84,38 +105,42 @@ def tile_picked_kjhingehopdmix_none_p_kernel(tc, x_words, x_scales, d_words, d_s
         nc.gpsimd.dma_start(gm_t[:], gm.rearrange("(p t) o -> p (t o)", t=PACK))
         nc.gpsimd.dma_start(gn_t[:], gn.rearrange("(p t) o -> p (t o)", t=PACK))
 
+        def deal_keys(dealt, picked):
+            nc.vector.tensor_copy(dealt[:].rearrange("p (t m) -> p m t", t=PACK), picked[:].rearrange("p (m t) -> p m t", t=PACK))
+
         ds_picked = sb("ds_picked", [P, H], U8)
         key_scales = sb("key_scales", [P, H], U8)
         nc.vector.tensor_copy(ds_picked[:], ds_table[:].indirect(k1_l[:]))
-        nc.vector.tensor_copy(key_scales[:].rearrange("p (t m) -> p m t", t=PACK), ds_picked[:].rearrange("p (m t) -> p m t", t=PACK))
+        deal_keys(key_scales, ds_picked)
         for j in range(1, 4):
-            nc.scalar.dma_start(key_scales[j:P:32, :].bitcast(I32), key_scales[8 * j : P : 32, :].bitcast(I32))
+            nc.scalar.dma_start(
+                key_scales[j:P:QUADRANT, :].bitcast(I32), key_scales[BLOCK_PARTITIONS * j : P : QUADRANT, :].bitcast(I32)
+            )
 
         xb_scales = sb("xb_scales", [P, S], U8)
         nc.vector.tensor_copy(xb_scales[:], xs_table[:].indirect(two_l[:]))
-        dw_picked = placed("dw_picked", [P, H], U32, 4 * G)
+        dw_picked = placed("dw_picked", [P, H], U32, PICKED_KEYS_AT)
         key_words = sb("key_words", [P, H], U32)
         nc.vector.tensor_copy(dw_picked[:], dw_table[:].indirect(k1_l[:]))
-        xb_words = placed("xb_words", [P, S], U32, 0)
+        xb_words = placed("xb_words", [P, S], U32, DICTIONARY_AT)
         nc.vector.tensor_copy(xb_words[:], xw_table[:].indirect(two_l[:]))
-        nc.vector.tensor_copy(key_words[:].rearrange("p (t m) -> p m t", t=PACK), dw_picked[:].rearrange("p (m t) -> p m t", t=PACK))
-        xa_words = placed("xa_words", [P, S], U32, 4 * G)
-        xa_scales = placed("xa_scales", [P, S], U8, 4 * S)
+        deal_keys(key_words, dw_picked)
+        xa_words = placed("xa_words", [P, S], U32, PICKED_KEYS_AT)
+        xa_scales = placed("xa_scales", [P, S], U8, DICTIONARY_AT + WORD_BYTES * S)
         nc.vector.tensor_copy(xa_words[:], xw_table[:].indirect(offs_l[:]))
         nc.vector.tensor_copy(xa_scales[:], xs_table[:].indirect(offs_l[:]))
 
-        def score(name, words, scales, windows):
-            pairs = []
+        def score(name, words, scales):
+            planes = []
             for t in range(PACK):
                 acc = bank(t, "%s_acc%d" % (name, t))
-                cols = slice(t * P, (t + 1) * P)
-                nc.tensor.matmul_mx(out=acc[:], lhsT=key_words[:, cols].bitcast(FP8X4), lhsT_scale=key_scales[:, cols],
-                                    rhs=words[:].bitcast(FP8X4), rhs_scale=scales[:], start=True, stop=True)
-                pairs.append((acc, windows[t]))
-            return pairs
-
-        def drain(pair, scale):
-            nc.scalar.activation(pair[1][:, 0:S], pair[0][:], ACT.Copy, scale=scale)
+                keys = slice(t * P, (t + 1) * P)
+                nc.tensor.matmul_mx(
+                    out=acc[:], lhsT=key_words[:, keys].bitcast(FP8X4), lhsT_scale=key_scales[:, keys],
+                    rhs=words[:].bitcast(FP8X4), rhs_scale=scales[:], start=True, stop=True,
+                )
+                planes.append(acc)
+            return planes
 
         b_scale = sb("b_scale", [P, PACK], F32)
         gm_safe = sb("gm_safe", [P, PACK], F32)
@@ -128,114 +153,116 @@ def tile_picked_kjhingehopdmix_none_p_kernel(tc, x_words, x_scales, d_words, d_s
         nc.vector.reciprocal(gm_recip[:], gm_safe[:])
         nc.gpsimd.tensor_scalar(gm_inverse[:], gm_recip[:], LARGE, -LARGE, ALU.min, ALU.max)
 
-        def interleave_view(ap):
+        def side_by_side(ap):
             return ap.rearrange("p (c i) t -> p c t i", i=2)
 
-        def plane_view(ap):
+        def by_planes(ap):
             return ap.rearrange("p t (c i) -> p c t i", i=2)
+
+        def quantise(name, rounded, width):
+            codes = sb(name + "_codes", [P, width], U32)
+            scales = sb(name + "_scales", [P, width], U8)
+            nc.vector.quantize_mx(out=codes[:].bitcast(FP8X4), scales=scales[:], in_=rounded[:].rearrange("p c t -> p (c t)"))
+            return codes, scales
 
         w1_il = sb("w1_il", [P, N, PACK], BF16)
         for h in range(2):
-            nc.scalar.activation(interleave_view(w1_il[:, h * HALF : (h + 1) * HALF, :]), plane_view(w1_raw[h][:]), ACT.Copy)
+            nc.scalar.activation(side_by_side(w1_il[:, halves[h], :]), by_planes(w1_raw[h][:]), ACT.Copy)
 
-        b_win = [placed("b_win%d" % t, [P, WINDOW], F32, B_WINDOWS + t * WINDOW_BYTES) for t in range(PACK)]
+        b_win = [placed("b_win%d" % t, [P, WINDOW], F32, B_WINDOWS_AT + t * WINDOW_BYTES) for t in range(PACK)]
         a_win = [sb("a_win%d" % t, [P, WINDOW], F32) for t in range(PACK)]
-        b_pairs = score("b", xb_words, xb_scales, b_win)
+        b_acc = score("b", xb_words, xb_scales)
         st_win = [sb("st_win%d" % t, [P, WINDOW], F32) for t in range(PACK)]
         g3 = [sb("g3_%d" % t, [P, S], F32) for t in range(PACK)]
-
         b_planes = sb("b_planes", [P, PACK, S], F32)
-
-        def drain_b(t):
-            drain(b_pairs[t], b_scale[:, t : t + 1])
-            nc.sync.dma_start(b_planes[:, t, :], b_win[t][:, 0:S])
-
-        def step(t):
-            nc.vector.tensor_tensor(st_win[t][:, 0:S], g3[t][:], b_win[t][:, 0:S], ALU.subtract)
 
         half_gn = sb("half_gn", [P, PACK], F32)
         nc.gpsimd.tensor_scalar(half_gn[:], gn_t[:], 0.5, 0.0, ALU.mult, ALU.add)
         up = sb("up", [P, PACK, S], F32)
         down = sb("down", [P, PACK, S], F32)
 
+        for t in range(PACK):
+            nc.scalar.activation(b_win[t][:, whole], b_acc[t][:], ACT.Copy, scale=b_scale[:, t : t + 1])
+            nc.sync.dma_start(b_planes[:, t, :], b_win[t][:, whole])
+        a_acc = score("a", xa_words, xa_scales)
+
+        def drain_a(t):
+            nc.scalar.activation(a_win[t][:, whole], a_acc[t][:], ACT.Copy, scale=SCORE_SCALE)
+
+        last = PACK - 1
+        drain_a(0)
+        nc.scalar.activation(g3[last][:, halves[1]], b_win[last][:].indirect(entries(n3_l, halves[1])), ACT.Copy)
+        for t in range(last):
+            nc.vector.tensor_copy(g3[t][:], b_win[t][:].indirect(n3_l[:]))
+        nc.vector.tensor_copy(g3[last][:, halves[0]], b_win[last][:].indirect(entries(n3_l, halves[0])))
+        for t in range(PACK):
+            nc.vector.tensor_tensor(st_win[t][:, whole], g3[t][:], b_win[t][:, whole], ALU.subtract)
+
         def a_step(t):
             g1 = sb("g1_%d" % t, [P, S], F32)
             g2 = sb("g2_%d" % t, [P, S], F32)
             nc.scalar.activation(g1[:], a_win[t][:].indirect(n1_l[:]), ACT.Copy)
-            if t + 1 < PACK:
-                drain(a_pairs[t + 1], SCORE_SCALE)
-            nc.scalar.activation(g2[:], a_win[t][:].indirect(n2_l[:]), ACT.Copy)
-            nc.vector.tensor_tensor(g1[:], a_win[t][:, 0:S], g1[:], ALU.subtract)
-            nc.vector.tensor_tensor(g2[:], g2[:], a_win[t][:, 0:S], ALU.subtract)
+            if t < last:
+                drain_a(t + 1)
+            if t == 0:
+                nc.vector.tensor_copy(g2[:], a_win[t][:].indirect(n2_l[:]))
+            else:
+                nc.scalar.activation(g2[:], a_win[t][:].indirect(n2_l[:]), ACT.Copy)
+            nc.vector.tensor_tensor(g1[:], a_win[t][:, whole], g1[:], ALU.subtract)
+            nc.vector.tensor_tensor(g2[:], g2[:], a_win[t][:, whole], ALU.subtract)
             nc.vector.tensor_scalar(down[:, t, :], g1[:], 0.0, gn_t[:, t : t + 1], ALU.max, ALU.mult)
             nc.vector.tensor_scalar(up[:, t, :], g2[:], 0.0, half_gn[:, t : t + 1], ALU.max, ALU.mult)
 
-        def quantise(name, il, width):
-            codes = sb(name + "_codes", [P, width], U32)
-            scales = sb(name + "_scales", [P, width], U8)
-            nc.vector.quantize_mx(out=codes[:].bitcast(FP8X4), scales=scales[:], in_=il[:].rearrange("p c t -> p (c t)"))
-            return codes, scales
-
-        for t in range(PACK):
-            drain_b(t)
-        a_pairs = score("a", xa_words, xa_scales, a_win)
-        drain(a_pairs[0], SCORE_SCALE)
-        nc.scalar.activation(g3[3][:, HALF:S], b_win[3][:].indirect(n3_l[:, HALF // 16 : S // 16]), ACT.Copy)
-        for t in range(3):
-            nc.vector.tensor_copy(g3[t][:], b_win[t][:].indirect(n3_l[:]))
-        nc.vector.tensor_copy(g3[3][:, 0:HALF], b_win[3][:].indirect(n3_l[:, 0 : HALF // 16]))
-        for t in range(PACK):
-            step(t)
         a_step(0)
         w1_q = quantise("w1", w1_il, N)
-        a_step(1)
-        a_step(2)
-        a_step(3)
+        for t in range(1, PACK):
+            a_step(t)
 
         z_il = sb("z_il", [P, S, PACK], BF16)
-        nc.vector.tensor_tensor(interleave_view(z_il[:]), plane_view(up[:]), plane_view(down[:]), ALU.add)
+        nc.vector.tensor_tensor(side_by_side(z_il[:]), by_planes(up[:]), by_planes(down[:]), ALU.add)
 
-        h_acc = [bank(PACK + m, "h_acc%d" % m) for m in range(4)]
-        h_win = [sb("h_win%d" % m, [P, WINDOW], F32) for m in range(4)]
+        h_acc = [bank(PACK + m, "h_acc%d" % m) for m in range(OUT_TILES)]
+        h_win = [sb("h_win%d" % m, [P, WINDOW], F32) for m in range(OUT_TILES)]
 
-        def h_pass(m, cols, w_q, w_first, z_pair, start, stop):
+        def h_pass(m, cols, w_q, w_first, moving, start, stop):
             rows = slice(m * P - w_first, (m + 1) * P - w_first)
-            nc.tensor.matmul_mx(out=h_acc[m][:, cols], lhsT=w_q[0][:, rows].bitcast(FP8X4), lhsT_scale=w_q[1][:, rows],
-                                rhs=z_pair[0][:].bitcast(FP8X4), rhs_scale=z_pair[1][:], start=start, stop=stop)
+            nc.tensor.matmul_mx(
+                out=h_acc[m][:, cols], lhsT=w_q[0][:, rows].bitcast(FP8X4), lhsT_scale=w_q[1][:, rows],
+                rhs=moving[0][:].bitcast(FP8X4), rhs_scale=moving[1][:], start=start, stop=stop,
+            )
 
         def gated_half(h):
             gates = sb("gates%d" % h, [P, PACK, HALF], F32)
             rounded = sb("z2_il%d" % h, [P, HALF, PACK], BF16)
             for t in range(PACK):
-                nc.scalar.activation(gates[:, t, :], st_win[t][:].indirect(n4_l[:, h * (HALF // 16) : (h + 1) * (HALF // 16)]), ACT.Sigmoid,
-                                     scale=gm_inverse[:, t : t + 1])
-            nc.vector.tensor_tensor(interleave_view(rounded[:]), plane_view(b_planes[:, :, h * HALF : (h + 1) * HALF]), plane_view(gates[:]), ALU.mult)
+                nc.scalar.activation(
+                    gates[:, t, :], st_win[t][:].indirect(entries(n4_l, halves[h])), ACT.Sigmoid, scale=gm_inverse[:, t : t + 1]
+                )
+            nc.vector.tensor_tensor(side_by_side(rounded[:]), by_planes(b_planes[:, :, halves[h]]), by_planes(gates[:]), ALU.mult)
             return rounded
 
-        whole = slice(0, S)
-        halves = [slice(0, HALF), slice(HALF, S)]
         z2_il = [gated_half(0)]
         z_q = quantise("z", z_il, S)
-        for m in range(4):
+        for m in range(OUT_TILES):
             h_pass(m, whole, w1_q, 0, z_q, True, False)
         z2_q = [quantise("z2_0", z2_il[0], HALF)]
         z2_il.append(gated_half(1))
-        w2_il = [sb("w2_il%d" % h, [P, HALF, PACK], BF16, tag="st_win%d" % (3 - h)) for h in range(2)]
+        w2_il = [sb("w2_il%d" % h, [P, HALF, PACK], BF16, tag="st_win%d" % (last - h)) for h in range(2)]
         for h in range(2):
-            nc.scalar.activation(interleave_view(w2_il[h][:]), plane_view(w2_raw[:, :, halves[h]]), ACT.Copy)
+            nc.scalar.activation(side_by_side(w2_il[h][:]), by_planes(w2_raw[:, :, halves[h]]), ACT.Copy)
         w2_q = [quantise("w2_0", w2_il[0], HALF)]
         z2_q.append(quantise("z2_1", z2_il[1], HALF))
         w2_q.append(quantise("w2_1", w2_il[1], HALF))
-        for m in range(4):
+        for m in range(OUT_TILES):
             for h in range(2):
-                h_pass(m, halves[h], w2_q[m // 2], (m // 2) * HALF, z2_q[h], False, h == 1)
+                h_pass(m, halves[h], w2_q[m * P // HALF], m * P // HALF * HALF, z2_q[h], False, h == 1)
 
-        g5 = [sb("g5_%d" % m, [P, S], F32) for m in range(4)]
-        g6 = [sb("g6_%d" % m, [P, S], F32) for m in range(4)]
-        g7 = [sb("g7_%d" % m, [P, S], F32) for m in range(4)]
+        g5 = [sb("g5_%d" % m, [P, S], F32) for m in range(OUT_TILES)]
+        g6 = [sb("g6_%d" % m, [P, S], F32) for m in range(OUT_TILES)]
+        g7 = [sb("g7_%d" % m, [P, S], F32) for m in range(OUT_TILES)]
 
         def fetch7(m):
-            nc.scalar.copy(h_win[m][:, 0:S], h_acc[m][:])
+            nc.scalar.copy(h_win[m][:, whole], h_acc[m][:])
             nc.vector.tensor_copy(g7[m][:], h_win[m][:].indirect(n7_l[:]))
 
         def larger67(m):
@@ -243,25 +270,27 @@ def tile_picked_kjhingehopdmix_none_p_kernel(tc, x_words, x_scales, d_words, d_s
             nc.vector.tensor_tensor(g6[m][:], g6[m][:], g7[m][:], ALU.max)
 
         def larger5(m, cols):
-            nc.scalar.activation(g5[m][:, cols], h_win[m][:].indirect(n5_l[:, cols.start // 16 : cols.stop // 16]), ACT.Copy)
+            nc.scalar.activation(g5[m][:, cols], h_win[m][:].indirect(entries(n5_l, cols)), ACT.Copy)
             nc.vector.tensor_tensor(g5[m][:, cols], h_win[m][:, cols], g5[m][:, cols], ALU.max)
 
         def finish(m, cols):
             nc.vector.tensor_tensor(g7[m][:, cols], g5[m][:, cols], g6[m][:, cols], ALU.subtract)
             nc.sync.dma_start(out[m * P : (m + 1) * P, cols], g7[m][:, cols])
 
-        fetch7(0)
-        fetch7(1)
-        for m in range(2):
+        ahead = 2
+        for m in range(ahead):
+            fetch7(m)
+        for m in range(OUT_TILES - ahead):
             larger67(m)
             larger5(m, whole)
-            fetch7(m + 2)
+            fetch7(m + ahead)
             finish(m, whole)
-        larger67(2)
-        larger5(2, whole)
-        larger67(3)
-        finish(2, whole)
+        before_end, end = OUT_TILES - 2, OUT_TILES - 1
+        larger67(before_end)
+        larger5(before_end, whole)
+        larger67(end)
+        finish(before_end, whole)
         for cols in halves:
-            larger5(3, cols)
+            larger5(end, cols)
         for cols in halves:
-            finish(3, cols)
+            finish(end, cols)

from contextlib import ExitStack

import concourse.mybir as mybir

K, T, S, N, G, H = 512, 1024, 512, 512, 2048, 512
FLOPS = 2 * (2 * K * H * S) + 2 * (2 * H * N * S)

F32 = mybir.dt.float32
BF16 = mybir.dt.bfloat16
I32 = mybir.dt.int32
U32 = mybir.dt.uint32
U16 = mybir.dt.uint16
U8 = mybir.dt.uint8
FP8X4 = mybir.dt.float8_e4m3fn_x4
ALU = mybir.AluOpType
ACT = mybir.ActivationFunctionType

P = 128
PACK = 4
QUADRANT = 32
BLOCK_PARTITIONS = 8
GROUP = 16
OUT_TILES = N // P
WINDOW = 2 * S
HALF = S // 2
SCORE_SCALE = 0.0625
LARGE = 2.0 ** 126

WORD_BYTES = 4
WINDOW_BYTES = WORD_BYTES * WINDOW
DICTIONARY_AT = 0
PICKED_KEYS_AT = DICTIONARY_AT + WORD_BYTES * G
B_WINDOWS_AT = PICKED_KEYS_AT + WORD_BYTES * H


def tile_picked_kjhingehopdmix_none_p_kernel(
    tc, x_words, x_scales, d_words, d_scales, gn, gm, w1, w2, offs, k1, two, n1, n2, n3, n4, n5, n6, n7, out
):
    nc = tc.nc
    with ExitStack() as ctx:
        keep = ctx.enter_context(tc.tile_pool(name="keep", bufs=1))
        reuse = ctx.enter_context(tc.tile_pool(name="reuse", bufs=1))
        psum = ctx.enter_context(tc.psum_pool(name="psum", bufs=1))

        def sb(name, shape, dtype, tag=""):
            return keep.tile(shape, dtype, name=name, tag=tag or name, align_bytes=64)

        def placed(name, shape, dtype, offset):
            return reuse.tile(shape, dtype, name=name, align_bytes=64, offset=offset)

        def load_list(name, dram):
            tile = keep.tile([P, S // GROUP], U16, name=name)
            nc.sync.dma_start(tile[:], dram)
            return tile

        def entries(lst, cols):
            return lst[:, cols.start // GROUP : cols.stop // GROUP]

        def bank(number, name):
            return psum.tile([P, S], F32, name=name, tag="bank%d" % number)

        whole = slice(0, S)
        halves = [slice(0, HALF), slice(HALF, S)]

        ds_table = sb("ds_table", [P, G], U8)
        xs_table = sb("xs_table", [P, T], U8)
        nc.vector.memset(ds_table[:].bitcast(I32), 0)
        warm_in = sb("warm_in", [P, 1], F32)
        warm_out = sb("warm_out", [P, 1], F32)
        nc.gpsimd.memset(warm_in[:], 0.0)
        nc.scalar.activation(warm_out[:], warm_in[:], ACT.Sigmoid)
        nc.vector.memset(xs_table[:].bitcast(I32), 0)

        xw_table = sb("xw_table", [P, T], U32)
        dw_table = placed("dw_table", [P, G], U32, DICTIONARY_AT)
        w1_rows = w1.rearrange("(p t) n -> p t n", t=PACK)
        w1_raw = [
            placed("w1_raw%d" % h, [P, PACK, HALF], F32, B_WINDOWS_AT + 2 * (1 - h) * WINDOW_BYTES + WINDOW_BYTES // 2)
            for h in range(2)
        ]
        w2_raw = sb("w2_raw", [P, PACK, N], F32)
        gn_t = sb("gn_t", [P, PACK], F32)
        gm_t = sb("gm_t", [P, PACK], F32)

        k1_l = load_list("k1_l", k1)
        nc.sync.dma_start(ds_table[0:P:BLOCK_PARTITIONS, :].bitcast(I32), d_scales[0].bitcast(I32))
        two_l = load_list("two_l", two)
        for q in range(P // QUADRANT):
            nc.sync.dma_start(
                xs_table[QUADRANT * q : QUADRANT * q + 4, :].bitcast(I32), x_scales[0, 4 * q : 4 * q + 4, :].bitcast(I32)
            )
        nc.sync.dma_start(dw_table[:].bitcast(I32), d_words[0].rearrange("p n t -> p (n t)").bitcast(I32))
        nc.sync.dma_start(xw_table[:].bitcast(I32), x_words[0].rearrange("p n t -> p (n t)").bitcast(I32))
        offs_l = load_list("offs_l", offs)
        for h in range(2):
            nc.sync.dma_start(w1_raw[h][:], w1_rows[:, :, halves[h]])
        n3_l = load_list("n3_l", n3)
        n1_l = load_list("n1_l", n1)
        n2_l = load_list("n2_l", n2)
        nc.sync.dma_start(w2_raw[:], w2.rearrange("(p t) n -> p t n", t=PACK))
        n4_l = load_list("n4_l", n4)
        n5_l = load_list("n5_l", n5)
        n6_l = load_list("n6_l", n6)
        n7_l = load_list("n7_l", n7)
        nc.gpsimd.dma_start(gm_t[:], gm.rearrange("(p t) o -> p (t o)", t=PACK))
        nc.gpsimd.dma_start(gn_t[:], gn.rearrange("(p t) o -> p (t o)", t=PACK))

        def deal_keys(dealt, picked):
            nc.vector.tensor_copy(dealt[:].rearrange("p (t m) -> p m t", t=PACK), picked[:].rearrange("p (m t) -> p m t", t=PACK))

        ds_picked = sb("ds_picked", [P, H], U8)
        key_scales = sb("key_scales", [P, H], U8)
        nc.vector.tensor_copy(ds_picked[:], ds_table[:].indirect(k1_l[:]))
        deal_keys(key_scales, ds_picked)
        for j in range(1, 4):
            nc.scalar.dma_start(
                key_scales[j:P:QUADRANT, :].bitcast(I32), key_scales[BLOCK_PARTITIONS * j : P : QUADRANT, :].bitcast(I32)
            )

        xb_scales = sb("xb_scales", [P, S], U8)
        nc.vector.tensor_copy(xb_scales[:], xs_table[:].indirect(two_l[:]))
        dw_picked = placed("dw_picked", [P, H], U32, PICKED_KEYS_AT)
        key_words = sb("key_words", [P, H], U32)
        nc.vector.tensor_copy(dw_picked[:], dw_table[:].indirect(k1_l[:]))
        xb_words = placed("xb_words", [P, S], U32, DICTIONARY_AT)
        nc.vector.tensor_copy(xb_words[:], xw_table[:].indirect(two_l[:]))
        deal_keys(key_words, dw_picked)
        xa_words = placed("xa_words", [P, S], U32, PICKED_KEYS_AT)
        xa_scales = placed("xa_scales", [P, S], U8, DICTIONARY_AT + WORD_BYTES * S)
        nc.vector.tensor_copy(xa_words[:], xw_table[:].indirect(offs_l[:]))
        nc.vector.tensor_copy(xa_scales[:], xs_table[:].indirect(offs_l[:]))

        def score(name, words, scales):
            planes = []
            for t in range(PACK):
                acc = bank(t, "%s_acc%d" % (name, t))
                keys = slice(t * P, (t + 1) * P)
                nc.tensor.matmul_mx(
                    out=acc[:], lhsT=key_words[:, keys].bitcast(FP8X4), lhsT_scale=key_scales[:, keys],
                    rhs=words[:].bitcast(FP8X4), rhs_scale=scales[:], start=True, stop=True,
                )
                planes.append(acc)
            return planes

        b_scale = sb("b_scale", [P, PACK], F32)
        gm_safe = sb("gm_safe", [P, PACK], F32)
        gm_inverse = sb("gm_inverse", [P, PACK], F32)
        gm_zero = sb("gm_zero", [P, PACK], F32)
        gm_recip = sb("gm_recip", [P, PACK], F32)
        nc.gpsimd.tensor_scalar(b_scale[:], gm_t[:], SCORE_SCALE, 0.0, ALU.mult, ALU.add)
        nc.gpsimd.tensor_scalar(gm_zero[:], gm_t[:], 0.0, 1.0, ALU.is_equal, ALU.mult)
        nc.gpsimd.tensor_tensor(gm_safe[:], gm_t[:], gm_zero[:], ALU.add)
        nc.vector.reciprocal(gm_recip[:], gm_safe[:])
        nc.gpsimd.tensor_scalar(gm_inverse[:], gm_recip[:], LARGE, -LARGE, ALU.min, ALU.max)

        def side_by_side(ap):
            return ap.rearrange("p (c i) t -> p c t i", i=2)

        def by_planes(ap):
            return ap.rearrange("p t (c i) -> p c t i", i=2)

        def quantise(name, rounded, width):
            codes = sb(name + "_codes", [P, width], U32)
            scales = sb(name + "_scales", [P, width], U8)
            nc.vector.quantize_mx(out=codes[:].bitcast(FP8X4), scales=scales[:], in_=rounded[:].rearrange("p c t -> p (c t)"))
            return codes, scales

        w1_il = sb("w1_il", [P, N, PACK], BF16)
        for h in range(2):
            nc.scalar.activation(side_by_side(w1_il[:, halves[h], :]), by_planes(w1_raw[h][:]), ACT.Copy)

        b_win = [placed("b_win%d" % t, [P, WINDOW], F32, B_WINDOWS_AT + t * WINDOW_BYTES) for t in range(PACK)]
        a_win = [sb("a_win%d" % t, [P, WINDOW], F32) for t in range(PACK)]
        b_acc = score("b", xb_words, xb_scales)
        st_win = [sb("st_win%d" % t, [P, WINDOW], F32) for t in range(PACK)]
        g3 = [sb("g3_%d" % t, [P, S], F32) for t in range(PACK)]
        b_planes = sb("b_planes", [P, PACK, S], F32)

        half_gn = sb("half_gn", [P, PACK], F32)
        nc.gpsimd.tensor_scalar(half_gn[:], gn_t[:], 0.5, 0.0, ALU.mult, ALU.add)
        up = sb("up", [P, PACK, S], F32)
        down = sb("down", [P, PACK, S], F32)

        for t in range(PACK):
            nc.scalar.activation(b_win[t][:, whole], b_acc[t][:], ACT.Copy, scale=b_scale[:, t : t + 1])
            nc.sync.dma_start(b_planes[:, t, :], b_win[t][:, whole])
        a_acc = score("a", xa_words, xa_scales)

        def drain_a(t):
            nc.scalar.activation(a_win[t][:, whole], a_acc[t][:], ACT.Copy, scale=SCORE_SCALE)

        last = PACK - 1
        drain_a(0)
        nc.scalar.activation(g3[last][:, halves[1]], b_win[last][:].indirect(entries(n3_l, halves[1])), ACT.Copy)
        for t in range(last):
            nc.vector.tensor_copy(g3[t][:], b_win[t][:].indirect(n3_l[:]))
        nc.vector.tensor_copy(g3[last][:, halves[0]], b_win[last][:].indirect(entries(n3_l, halves[0])))
        for t in range(PACK):
            nc.vector.tensor_tensor(st_win[t][:, whole], g3[t][:], b_win[t][:, whole], ALU.subtract)

        def a_step(t):
            g1 = sb("g1_%d" % t, [P, S], F32)
            g2 = sb("g2_%d" % t, [P, S], F32)
            nc.scalar.activation(g1[:], a_win[t][:].indirect(n1_l[:]), ACT.Copy)
            if t < last:
                drain_a(t + 1)
            if t == 0:
                nc.vector.tensor_copy(g2[:], a_win[t][:].indirect(n2_l[:]))
            else:
                nc.scalar.activation(g2[:], a_win[t][:].indirect(n2_l[:]), ACT.Copy)
            nc.vector.tensor_tensor(g1[:], a_win[t][:, whole], g1[:], ALU.subtract)
            nc.vector.tensor_tensor(g2[:], g2[:], a_win[t][:, whole], ALU.subtract)
            nc.vector.tensor_scalar(down[:, t, :], g1[:], 0.0, gn_t[:, t : t + 1], ALU.max, ALU.mult)
            nc.vector.tensor_scalar(up[:, t, :], g2[:], 0.0, half_gn[:, t : t + 1], ALU.max, ALU.mult)

        a_step(0)
        w1_q = quantise("w1", w1_il, N)
        for t in range(1, PACK):
            a_step(t)

        z_il = sb("z_il", [P, S, PACK], BF16)
        nc.vector.tensor_tensor(side_by_side(z_il[:]), by_planes(up[:]), by_planes(down[:]), ALU.add)

        h_acc = [bank(PACK + m, "h_acc%d" % m) for m in range(OUT_TILES)]
        h_win = [sb("h_win%d" % m, [P, WINDOW], F32) for m in range(OUT_TILES)]

        def h_pass(m, cols, w_q, w_first, moving, start, stop):
            rows = slice(m * P - w_first, (m + 1) * P - w_first)
            nc.tensor.matmul_mx(
                out=h_acc[m][:, cols], lhsT=w_q[0][:, rows].bitcast(FP8X4), lhsT_scale=w_q[1][:, rows],
                rhs=moving[0][:].bitcast(FP8X4), rhs_scale=moving[1][:], start=start, stop=stop,
            )

        def gated_half(h):
            gates = sb("gates%d" % h, [P, PACK, HALF], F32)
            rounded = sb("z2_il%d" % h, [P, HALF, PACK], BF16)
            for t in range(PACK):
                nc.scalar.activation(
                    gates[:, t, :], st_win[t][:].indirect(entries(n4_l, halves[h])), ACT.Sigmoid, scale=gm_inverse[:, t : t + 1]
                )
            nc.vector.tensor_tensor(side_by_side(rounded[:]), by_planes(b_planes[:, :, halves[h]]), by_planes(gates[:]), ALU.mult)
            return rounded

        z2_il = [gated_half(0)]
        z_q = quantise("z", z_il, S)
        for m in range(OUT_TILES):
            h_pass(m, whole, w1_q, 0, z_q, True, False)
        z2_q = [quantise("z2_0", z2_il[0], HALF)]
        z2_il.append(gated_half(1))
        w2_il = [sb("w2_il%d" % h, [P, HALF, PACK], BF16, tag="st_win%d" % (last - h)) for h in range(2)]
        for h in range(2):
            nc.scalar.activation(side_by_side(w2_il[h][:]), by_planes(w2_raw[:, :, halves[h]]), ACT.Copy)
        w2_q = [quantise("w2_0", w2_il[0], HALF)]
        z2_q.append(quantise("z2_1", z2_il[1], HALF))
        w2_q.append(quantise("w2_1", w2_il[1], HALF))
        for m in range(OUT_TILES):
            for h in range(2):
                h_pass(m, halves[h], w2_q[m * P // HALF], m * P // HALF * HALF, z2_q[h], False, h == 1)

        g5 = [sb("g5_%d" % m, [P, S], F32) for m in range(OUT_TILES)]
        g6 = [sb("g6_%d" % m, [P, S], F32) for m in range(OUT_TILES)]
        g7 = [sb("g7_%d" % m, [P, S], F32) for m in range(OUT_TILES)]

        def fetch7(m):
            nc.scalar.copy(h_win[m][:, whole], h_acc[m][:])
            nc.vector.tensor_copy(g7[m][:], h_win[m][:].indirect(n7_l[:]))

        def larger67(m):
            nc.scalar.activation(g6[m][:], h_win[m][:].indirect(n6_l[:]), ACT.Copy)
            nc.vector.tensor_tensor(g6[m][:], g6[m][:], g7[m][:], ALU.max)

        def larger5(m, cols):
            nc.scalar.activation(g5[m][:, cols], h_win[m][:].indirect(entries(n5_l, cols)), ACT.Copy)
            nc.vector.tensor_tensor(g5[m][:, cols], h_win[m][:, cols], g5[m][:, cols], ALU.max)

        def finish(m, cols):
            nc.vector.tensor_tensor(g7[m][:, cols], g5[m][:, cols], g6[m][:, cols], ALU.subtract)
            nc.sync.dma_start(out[m * P : (m + 1) * P, cols], g7[m][:, cols])

        ahead = 2
        for m in range(ahead):
            fetch7(m)
        for m in range(OUT_TILES - ahead):
            larger67(m)
            larger5(m, whole)
            fetch7(m + ahead)
            finish(m, whole)
        before_end, end = OUT_TILES - 2, OUT_TILES - 1
        larger67(before_end)
        larger5(before_end, whole)
        larger67(end)
        finish(before_end, whole)
        for cols in halves:
            larger5(end, cols)
        for cols in halves:
            finish(end, cols)
